import numpy as np
import ml_dtypes


def mxq(x, axis, fmt="e4m3"):
    dtype, down = {"e4m3": (ml_dtypes.float8_e4m3fn, 7), "e5m2": (ml_dtypes.float8_e5m2, 14)}[fmt]
    v = np.moveaxis(np.asarray(x, np.float32).astype(ml_dtypes.bfloat16).astype(np.float64), axis, -1)
    blocks = v.reshape(v.shape[:-1] + (-1, 32))
    amax = np.abs(blocks).max(-1, keepdims=True)
    byte = np.maximum(np.where(amax > 0, np.frexp(amax)[1] - 1 + 127, 0) - down, 1)
    scale = np.exp2(byte - 127.0)
    codes = (blocks / scale).astype(np.float32).astype(dtype).astype(np.float64)
    return np.moveaxis((codes * scale).reshape(v.shape), -1, axis)


WIDE = False


def mx_kscale(k):
    if not WIDE:
        return np.ones(k)
    levels = np.array([10, -10, 5, -5, 0])
    if k % 512:
        return np.exp2(np.random.permutation(np.resize(levels, k // 32))).repeat(32)
    a = np.empty((k // 512, 16))
    for p in range(k // 512):
        a[p, :8] = np.random.permutation(np.resize(levels, 8))
        for g in range(8):
            far = levels[np.abs(levels - a[p, g]) >= 10]
            a[p, g + 8] = far[np.random.randint(len(far))]
    return np.exp2(a.ravel()).repeat(32)


def f64(x):
    return np.asarray(x).astype(np.float64)


def striped(idx):
    return np.tile(idx.reshape(-1, 16).T, (8, 1)).astype(np.uint16)


def unstriped(offs):
    return offs[:16].T.reshape(-1).astype(np.int64)


def gelu(v):
    return 0.5 * v * (1.0 + np.tanh(np.sqrt(2.0 / np.pi) * (v + 0.044715 * v**3)))


K, T, S, N = 1024, 1024, 512, 256
P = 2 ** 7


def setup_inputs():
    n = np.random.standard_normal
    s = mx_kscale(K)[:, None]
    return {
        "xT": (n((K, T)) * s).astype(np.float32),
        "zp": np.tile(np.random.uniform(-0.6, 0.6, T), (P, 1)).astype(np.float32),
        "csum": n((N, 1)).astype(np.float32),
        "w1": (n((K, N)) / np.sqrt(K) / s).astype(np.float32),
        "offs": striped(np.random.permutation(T)[:S]),
    }


def reference(xT, zp, csum, w1, offs):
    xq = mxq(f64(xT)[:, unstriped(offs)], 0, "e4m3")
    y = mxq(f64(w1), 0, "e4m3").T @ xq
    zg = f64(zp)[:1][:, unstriped(offs)]
    return gelu(y - (f64(csum) * zg))

@@ -1,0 +1,215 @@
+from contextlib import ExitStack
+
+import concourse.mybir as mybir
+from concourse.masks import make_identity
+
+K, T, S, N = 1024, 1024, 512, 256
+FLOPS = 2 * K * S * N
+
+F32 = mybir.dt.float32
+BF16 = mybir.dt.bfloat16
+I32 = mybir.dt.int32
+U32 = mybir.dt.uint32
+U16 = mybir.dt.uint16
+U8 = mybir.dt.uint8
+FP8X4 = mybir.dt.float8_e4m3fn_x4
+GELU = mybir.ActivationFunctionType.Gelu_apprx_tanh
+MULT = mybir.AluOpType.mult
+SUBTRACT = mybir.AluOpType.subtract
+
+P = 128
+PACK = 4
+K_PASS = P * PACK
+PASSES = K // K_PASS
+BLOCKS = N // P
+VECTOR_COLS = (672, 672, 672, 672)
+EARLY = ((0, 256), (256, 512))
+LATE = ((0, 256), (256, 384), (384, 512))
+
+
+def tile_picked_zeropt_gelu_l_kernel(tc, xT, zp, csum, w1, offs, out):
+    nc = tc.nc
+    with ExitStack() as ctx:
+        keep = ctx.enter_context(tc.tile_pool(name="keep", bufs=1))
+        psum = ctx.enter_context(tc.psum_pool(name="psum", bufs=1))
+
+        def tile(name, shape, dtype, tag=None):
+            return keep.tile(shape, dtype, name=name, tag=tag or name, align_bytes=64)
+
+        offsets = keep.tile([P, S // 16], U16, name="offsets")
+        zp_table = tile("zp_table", [P, T], F32)
+        nc.gpsimd.memset(zp_table[0 : P - 1, :], 0.0)
+        nc.scalar.dma_start(zp_table[P - 1 : P, :], zp[0:1, :])
+        nc.sync.dma_start(offsets[:], offs)
+        x_rows = xT.rearrange("(g p u t) c -> g u p t c", g=PASSES, u=2, t=2)
+        w_rows = w1.rearrange("(g p j) m -> g p j m", g=PASSES, j=PACK)
+        x_raw = {}
+        w_raw = {}
+
+        def load_x(g, u):
+            x_raw[g, u] = tile("x_raw%d%d" % (g, u), [P, 2, T], F32)
+            nc.sync.dma_start(x_raw[g, u][:], x_rows[g, u])
+
+        def load_w(g):
+            w_raw[g] = tile("w_raw%d" % g, [P, PACK, N], F32)
+            nc.sync.dma_start(w_raw[g][:], w_rows[g])
+
+        load_x(0, 0)
+        load_x(0, 1)
+        load_x(1, 0)
+        load_w(0)
+        load_x(1, 1)
+        load_w(1)
+        weight = tile("weight", [P, BLOCKS], F32)
+        with nc.allow_non_contiguous_dma(reason="one value a partition"):
+            nc.sync.dma_start(weight[:], csum.rearrange("(b p) o -> p (b o)", p=P))
+
+        zero = tile("zero", [P, 1], F32)
+        nc.vector.memset(zero[:], 0.0)
+        no_bias = tile("no_bias", [P, 1], F32)
+        nc.scalar.activation(no_bias[:], zero[:], GELU)
+
+        identity = tile("identity", [P, P], F32)
+        make_identity(nc, identity[:])
+        zp_row = tile("zp_row", [P, S], F32)
+        nc.vector.tensor_copy(zp_row[:], zp_table[:].indirect(offsets[:]))
+        turned = psum.tile([P, S // P, P], F32, name="turned")
+        for c in range(S // P):
+            nc.tensor.transpose(turned[:, c, :], zp_row[:, c * P : (c + 1) * P], identity[:])
+        zp_cols = tile("zp_cols", [P, S // P], F32)
+        nc.scalar.copy(zp_cols[:], turned[:, :, P - 1])
+        spread = psum.tile([P, S // P, P], F32, name="spread")
+        for c in range(S // P):
+            nc.tensor.transpose(spread[:, c, :], zp_cols[:, c : c + 1].to_broadcast([P, P]), identity[:])
+        zp_picked = tile("zp_picked", [P, S], F32)
+        nc.scalar.copy(zp_picked[:], spread[:].rearrange("p c n -> p (c n)"))
+
+        picked = {}
+        woven = {}
+        x_codes = {}
+        x_scales = {}
+        w_grouped = {}
+        w_codes = {}
+        w_scales = {}
+        acc = {}
+
+        def round_pairs(g, u):
+            table = tile("table%d%d" % (g, u), [P, T], U32)
+            pairs = table[:].bitcast(BF16).rearrange("p (c t) -> p c t", t=2)
+            src = x_raw[g, u][:].rearrange("p t c -> p c t")
+            split = VECTOR_COLS[2 * g + u]
+            nc.scalar.copy(pairs[:, split:, :], src[:, split:, :])
+            nc.vector.tensor_copy(pairs[:, :split, :], src[:, :split, :])
+            return table
+
+        def gather(g, u, piece, table):
+            lo, hi = piece
+            if u == 0:
+                picked[g, piece] = tile("picked%d_%d" % (g, lo), [P, 2, hi - lo], U32)
+            nc.vector.tensor_copy(picked[g, piece][:, u, :], table[:].indirect(offsets[:, lo // 16 : hi // 16]))
+
+        def weave(g, piece, on_scalar, dst=None):
+            lo, hi = piece
+            if dst is None:
+                dst = tile("woven%d_%d" % (g, lo), [P, hi - lo, 2], U32)[:]
+            woven[g, piece] = dst
+            src = picked[g, piece][:]
+            if on_scalar:
+                nc.scalar.copy(dst, src.rearrange("p u s -> p s u"))
+            else:
+                nc.vector.tensor_copy(dst.bitcast(I32), src.bitcast(I32).rearrange("p u s -> p s u"))
+
+        def quantise_x(g, piece):
+            lo, hi = piece
+            codes = tile("x_codes%d_%d" % (g, lo), [P, hi - lo], U32)
+            scales = tile("x_scales%d_%d" % (g, lo), [P, hi - lo], U8)
+            nc.vector.quantize_mx(
+                out=codes[:].bitcast(FP8X4),
+                scales=scales[:],
+                in_=woven[g, piece].rearrange("p s u -> p (s u)").bitcast(BF16),
+            )
+            for a, b in LATE:
+                if lo <= a and b <= hi:
+                    x_codes[g, (a, b)] = codes[:, a - lo : b - lo]
+                    x_scales[g, (a, b)] = scales[:, a - lo : b - lo]
+
+        def round_w(g, b, engine):
+            w_grouped[g, b] = tile("w_grouped%d%d" % (g, b), [P, P, PACK], BF16)
+            dst = w_grouped[g, b][:].rearrange("p (c i) j -> p c j i", i=4)
+            src = w_raw[g][:, :, b * P : (b + 1) * P].rearrange("p j (c i) -> p c j i", i=4)
+            if engine == "scalar":
+                nc.scalar.copy(dst, src)
+            elif engine == "vector":
+                nc.vector.tensor_copy(dst, src)
+            else:
+                nc.gpsimd.tensor_copy(dst, src)
+
+        def quantise_w(g, b):
+            w_codes[g, b] = tile("w_codes%d%d" % (g, b), [P, P], U32)
+            w_scales[g, b] = tile("w_scales%d%d" % (g, b), [P, P], U8)
+            nc.vector.quantize_mx(
+                out=w_codes[g, b][:].bitcast(FP8X4),
+                scales=w_scales[g, b][:],
+                in_=w_grouped[g, b][:].rearrange("p m j -> p (m j)"),
+            )
+
+        def multiply(g, piece, b):
+            lo, hi = piece
+            if g == 0:
+                acc[b, piece] = psum.tile([P, hi - lo], F32, name="acc%d_%d" % (b, lo))
+            nc.tensor.matmul_mx(
+                out=acc[b, piece][:],
+                lhsT=w_codes[g, b][:].bitcast(FP8X4),
+                lhsT_scale=w_scales[g, b][:],
+                rhs=x_codes[g, piece].bitcast(FP8X4),
+                rhs_scale=x_scales[g, piece],
+                start=(g == 0),
+                stop=(g == PASSES - 1),
+            )
+
+        def finish(piece, b):
+            lo, hi = piece
+            negated = tile("negated%d_%d" % (b, lo), [P, hi - lo], F32)
+            nc.vector.scalar_tensor_tensor(
+                negated[:], zp_picked[:, lo:hi], weight[:, b : b + 1], acc[b, piece][:], MULT, SUBTRACT
+            )
+            result = tile("result%d_%d" % (b, lo), [P, hi - lo], F32)
+            nc.scalar.activation(result[:], negated[:], GELU, bias=no_bias[:], scale=-1.0)
+            nc.sync.dma_start(out[b * P : (b + 1) * P, lo:hi], result[:])
+
+        for u in range(2):
+            table = round_pairs(0, u)
+            for piece in EARLY:
+                gather(0, u, piece, table)
+        table = round_pairs(1, 0)
+        for piece in LATE:
+            gather(1, 0, piece, table)
+        woven0 = tile("woven0", [P, S, 2], U32, tag="x_raw10")
+        for lo, hi in EARLY:
+            weave(0, (lo, hi), True, woven0[:, lo:hi, :])
+            quantise_x(0, (lo, hi))
+        for b in range(BLOCKS):
+            round_w(0, b, "scalar")
+            quantise_w(0, b)
+        for b in range(BLOCKS):
+            for piece in LATE:
+                multiply(0, piece, b)
+        table = round_pairs(1, 1)
+        for piece in LATE:
+            gather(1, 1, piece, table)
+        for b in range(BLOCKS):
+            round_w(1, b, "scalar")
+        weave(1, LATE[0], False)
+        weave(1, LATE[1], False)
+        weave(1, LATE[2], True)
+        quantise_w(1, 0)
+        quantise_x(1, LATE[0])
+        quantise_w(1, 1)
+        quantise_x(1, LATE[1])
+        quantise_x(1, LATE[2])
+        for piece in LATE:
+            for b in range(BLOCKS):
+                multiply(1, piece, b)
+        for piece in LATE:
+            for b in range(BLOCKS):
+                finish(piece, b)

@@ -22,9 +22,9 @@ PACK = 4
 K_PASS = P * PACK
 PASSES = K // K_PASS
 BLOCKS = N // P
-VECTOR_COLS = (672, 672, 672, 672)
-EARLY = ((0, 256), (256, 512))
-LATE = ((0, 256), (256, 384), (384, 512))
+VECTOR_COLS = (672, 672, 608, 688)
+WHOLE = (0, S)
+LATE = ((0, 256), (256, 512))
 
 
 def tile_picked_zeropt_gelu_l_kernel(tc, xT, zp, csum, w1, offs, out):
@@ -39,7 +39,7 @@ def tile_picked_zeropt_gelu_l_kernel(tc, xT, zp, csum, w1, offs, out):
         offsets = keep.tile([P, S // 16], U16, name="offsets")
         zp_table = tile("zp_table", [P, T], F32)
         nc.gpsimd.memset(zp_table[0 : P - 1, :], 0.0)
-        nc.scalar.dma_start(zp_table[P - 1 : P, :], zp[0:1, :])
+        nc.sync.dma_start(zp_table[P - 1 : P, :], zp[0:1, :])
         nc.sync.dma_start(offsets[:], offs)
         x_rows = xT.rearrange("(g p u t) c -> g u p t c", g=PASSES, u=2, t=2)
         w_rows = w1.rearrange("(g p j) m -> g p j m", g=PASSES, j=PACK)
@@ -81,21 +81,17 @@ def tile_picked_zeropt_gelu_l_kernel(tc, xT, zp, csum, w1, offs, out):
         spread = psum.tile([P, S // P, P], F32, name="spread")
         for c in range(S // P):
             nc.tensor.transpose(spread[:, c, :], zp_cols[:, c : c + 1].to_broadcast([P, P]), identity[:])
-        zp_picked = tile("zp_picked", [P, S], F32)
-        nc.scalar.copy(zp_picked[:], spread[:].rearrange("p c n -> p (c n)"))
 
         picked = {}
         woven = {}
         x_codes = {}
         x_scales = {}
-        w_grouped = {}
         w_codes = {}
         w_scales = {}
         acc = {}
 
-        def round_pairs(g, u):
-            table = tile("table%d%d" % (g, u), [P, T], U32)
-            pairs = table[:].bitcast(BF16).rearrange("p (c t) -> p c t", t=2)
+        def round_pairs(g, u, table):
+            pairs = table.bitcast(BF16).rearrange("p (c t) -> p c t", t=2)
             src = x_raw[g, u][:].rearrange("p t c -> p c t")
             split = VECTOR_COLS[2 * g + u]
             nc.scalar.copy(pairs[:, split:, :], src[:, split:, :])
@@ -106,7 +102,7 @@ def tile_picked_zeropt_gelu_l_kernel(tc, xT, zp, csum, w1, offs, out):
             lo, hi = piece
             if u == 0:
                 picked[g, piece] = tile("picked%d_%d" % (g, lo), [P, 2, hi - lo], U32)
-            nc.vector.tensor_copy(picked[g, piece][:, u, :], table[:].indirect(offsets[:, lo // 16 : hi // 16]))
+            nc.vector.tensor_copy(picked[g, piece][:, u, :], table.indirect(offsets[:, lo // 16 : hi // 16]))
 
         def weave(g, piece, on_scalar, dst=None):
             lo, hi = piece
@@ -119,9 +115,9 @@ def tile_picked_zeropt_gelu_l_kernel(tc, xT, zp, csum, w1, offs, out):
             else:
                 nc.vector.tensor_copy(dst.bitcast(I32), src.bitcast(I32).rearrange("p u s -> p s u"))
 
-        def quantise_x(g, piece):
+        def quantise_x(g, piece, tag=None):
             lo, hi = piece
-            codes = tile("x_codes%d_%d" % (g, lo), [P, hi - lo], U32)
+            codes = tile("x_codes%d_%d" % (g, lo), [P, hi - lo], U32, tag=tag)
             scales = tile("x_scales%d_%d" % (g, lo), [P, hi - lo], U8)
             nc.vector.quantize_mx(
                 out=codes[:].bitcast(FP8X4),
@@ -133,10 +129,9 @@ def tile_picked_zeropt_gelu_l_kernel(tc, xT, zp, csum, w1, offs, out):
                     x_codes[g, (a, b)] = codes[:, a - lo : b - lo]
                     x_scales[g, (a, b)] = scales[:, a - lo : b - lo]
 
-        def round_w(g, b, engine):
-            w_grouped[g, b] = tile("w_grouped%d%d" % (g, b), [P, P, PACK], BF16)
-            dst = w_grouped[g, b][:].rearrange("p (c i) j -> p c j i", i=4)
-            src = w_raw[g][:, :, b * P : (b + 1) * P].rearrange("p j (c i) -> p c j i", i=4)
+        def round_w(g, lo, hi, engine, grouped):
+            dst = grouped[:, lo:hi, :].rearrange("p (c i) j -> p c j i", i=4)
+            src = w_raw[g][:, :, lo:hi].rearrange("p j (c i) -> p c j i", i=4)
             if engine == "scalar":
                 nc.scalar.copy(dst, src)
             elif engine == "vector":
@@ -144,14 +139,17 @@ def tile_picked_zeropt_gelu_l_kernel(tc, xT, zp, csum, w1, offs, out):
             else:
                 nc.gpsimd.tensor_copy(dst, src)
 
-        def quantise_w(g, b):
-            w_codes[g, b] = tile("w_codes%d%d" % (g, b), [P, P], U32)
-            w_scales[g, b] = tile("w_scales%d%d" % (g, b), [P, P], U8)
+        def quantise_w(g, lo, hi, grouped, tag=None):
+            codes = tile("w_codes%d_%d" % (g, lo), [P, hi - lo], U32, tag=tag)
+            scales = tile("w_scales%d_%d" % (g, lo), [P, hi - lo], U8)
             nc.vector.quantize_mx(
-                out=w_codes[g, b][:].bitcast(FP8X4),
-                scales=w_scales[g, b][:],
-                in_=w_grouped[g, b][:].rearrange("p m j -> p (m j)"),
+                out=codes[:].bitcast(FP8X4),
+                scales=scales[:],
+                in_=grouped[:, lo:hi, :].rearrange("p m j -> p (m j)"),
             )
+            for m in range(lo, hi, P):
+                w_codes[g, m // P] = codes[:, m - lo : m - lo + P]
+                w_scales[g, m // P] = scales[:, m - lo : m - lo + P]
 
         def multiply(g, piece, b):
             lo, hi = piece
@@ -159,8 +157,8 @@ def tile_picked_zeropt_gelu_l_kernel(tc, xT, zp, csum, w1, offs, out):
                 acc[b, piece] = psum.tile([P, hi - lo], F32, name="acc%d_%d" % (b, lo))
             nc.tensor.matmul_mx(
                 out=acc[b, piece][:],
-                lhsT=w_codes[g, b][:].bitcast(FP8X4),
-                lhsT_scale=w_scales[g, b][:],
+                lhsT=w_codes[g, b].bitcast(FP8X4),
+                lhsT_scale=w_scales[g, b],
                 rhs=x_codes[g, piece].bitcast(FP8X4),
                 rhs_scale=x_scales[g, piece],
                 start=(g == 0),
@@ -177,36 +175,33 @@ def tile_picked_zeropt_gelu_l_kernel(tc, xT, zp, csum, w1, offs, out):
             nc.scalar.activation(result[:], negated[:], GELU, bias=no_bias[:], scale=-1.0)
             nc.sync.dma_start(out[b * P : (b + 1) * P, lo:hi], result[:])
 
-        for u in range(2):
-            table = round_pairs(0, u)
-            for piece in EARLY:
-                gather(0, u, piece, table)
-        table = round_pairs(1, 0)
+        table = round_pairs(0, 0, tile("table00", [P, T], U32)[:])
+        gather(0, 0, WHOLE, table)
+        table = round_pairs(0, 1, tile("table01", [P, T], U32)[:])
+        zp_picked = tile("zp_picked", [P, S], F32, tag="table00")
+        nc.scalar.copy(zp_picked[:], spread[:].rearrange("p c n -> p (c n)"))
+        gather(0, 1, WHOLE, table)
+        table = round_pairs(1, 0, tile("table10", [P, T], U32)[:])
         for piece in LATE:
             gather(1, 0, piece, table)
-        woven0 = tile("woven0", [P, S, 2], U32, tag="x_raw10")
-        for lo, hi in EARLY:
-            weave(0, (lo, hi), True, woven0[:, lo:hi, :])
-            quantise_x(0, (lo, hi))
-        for b in range(BLOCKS):
-            round_w(0, b, "scalar")
-            quantise_w(0, b)
+        weave(0, WHOLE, True, tile("woven0", [P, S, 2], U32, tag="x_raw10")[:])
+        quantise_x(0, WHOLE)
+        grouped = tile("w_grouped0", [P, N, PACK], BF16)[:]
+        round_w(0, 0, N, "scalar", grouped)
+        quantise_w(0, 0, N, grouped)
         for b in range(BLOCKS):
             for piece in LATE:
                 multiply(0, piece, b)
-        table = round_pairs(1, 1)
+        table = round_pairs(1, 1, tile("table11", [P, T], U32)[:])
         for piece in LATE:
             gather(1, 1, piece, table)
-        for b in range(BLOCKS):
-            round_w(1, b, "scalar")
+        grouped = tile("w_grouped1", [P, N, PACK], BF16)[:]
+        round_w(1, 0, N, "scalar", grouped)
         weave(1, LATE[0], False)
-        weave(1, LATE[1], False)
-        weave(1, LATE[2], True)
-        quantise_w(1, 0)
-        quantise_x(1, LATE[0])
-        quantise_w(1, 1)
+        weave(1, LATE[1], True)
+        quantise_w(1, 0, N, grouped)
+        quantise_x(1, LATE[0], tag="w_raw1")
         quantise_x(1, LATE[1])
-        quantise_x(1, LATE[2])
         for piece in LATE:
             for b in range(BLOCKS):
                 multiply(1, piece, b)

@@ -22,7 +22,7 @@ PACK = 4
 K_PASS = P * PACK
 PASSES = K // K_PASS
 BLOCKS = N // P
-VECTOR_COLS = (672, 672, 608, 688)
+VECTOR_COLS = (672, 672, 608, 736)
 WHOLE = (0, S)
 LATE = ((0, 256), (256, 512))
 
@@ -39,7 +39,7 @@ def tile_picked_zeropt_gelu_l_kernel(tc, xT, zp, csum, w1, offs, out):
         offsets = keep.tile([P, S // 16], U16, name="offsets")
         zp_table = tile("zp_table", [P, T], F32)
         nc.gpsimd.memset(zp_table[0 : P - 1, :], 0.0)
-        nc.sync.dma_start(zp_table[P - 1 : P, :], zp[0:1, :])
+        nc.scalar.dma_start(zp_table[P - 1 : P, :], zp[0:1, :])
         nc.sync.dma_start(offsets[:], offs)
         x_rows = xT.rearrange("(g p u t) c -> g u p t c", g=PASSES, u=2, t=2)
         w_rows = w1.rearrange("(g p j) m -> g p j m", g=PASSES, j=PACK)
@@ -50,6 +50,14 @@ def tile_picked_zeropt_gelu_l_kernel(tc, xT, zp, csum, w1, offs, out):
             x_raw[g, u] = tile("x_raw%d%d" % (g, u), [P, 2, T], F32)
             nc.sync.dma_start(x_raw[g, u][:], x_rows[g, u])
 
+        def load_x_in_two(g, u):
+            split = VECTOR_COLS[2 * g + u]
+            x_raw[g, u] = []
+            for lo, hi in ((0, split), (split, T)):
+                part = tile("x_raw%d%d_%d" % (g, u, lo), [P, 2, hi - lo], F32)
+                nc.sync.dma_start(part[:], x_rows[g, u][:, :, lo:hi])
+                x_raw[g, u].append(part)
+
         def load_w(g):
             w_raw[g] = tile("w_raw%d" % g, [P, PACK, N], F32)
             nc.sync.dma_start(w_raw[g][:], w_rows[g])
@@ -58,7 +66,7 @@ def tile_picked_zeropt_gelu_l_kernel(tc, xT, zp, csum, w1, offs, out):
         load_x(0, 1)
         load_x(1, 0)
         load_w(0)
-        load_x(1, 1)
+        load_x_in_two(1, 1)
         load_w(1)
         weight = tile("weight", [P, BLOCKS], F32)
         with nc.allow_non_contiguous_dma(reason="one value a partition"):
@@ -96,6 +104,14 @@ def tile_picked_zeropt_gelu_l_kernel(tc, xT, zp, csum, w1, offs, out):
             split = VECTOR_COLS[2 * g + u]
             nc.scalar.copy(pairs[:, split:, :], src[:, split:, :])
             nc.vector.tensor_copy(pairs[:, :split, :], src[:, :split, :])
+            return table
+
+        def round_pairs_in_two(g, u, table):
+            pairs = table.bitcast(BF16).rearrange("p (c t) -> p c t", t=2)
+            split = VECTOR_COLS[2 * g + u]
+            first, second = x_raw[g, u]
+            nc.vector.tensor_copy(pairs[:, :split, :], first[:].rearrange("p t c -> p c t"))
+            nc.scalar.copy(pairs[:, split:, :], second[:].rearrange("p t c -> p c t"))
             return table
 
         def gather(g, u, piece, table):
@@ -165,11 +181,10 @@ def tile_picked_zeropt_gelu_l_kernel(tc, xT, zp, csum, w1, offs, out):
                 stop=(g == PASSES - 1),
             )
 
-        def finish(piece, b):
-            lo, hi = piece
+        def finish(piece, b, lo, hi):
             negated = tile("negated%d_%d" % (b, lo), [P, hi - lo], F32)
             nc.vector.scalar_tensor_tensor(
-                negated[:], zp_picked[:, lo:hi], weight[:, b : b + 1], acc[b, piece][:], MULT, SUBTRACT
+                negated[:], zp_picked[:, lo:hi], weight[:, b : b + 1], acc[b, piece][:, lo - piece[0] : hi - piece[0]], MULT, SUBTRACT
             )
             result = tile("result%d_%d" % (b, lo), [P, hi - lo], F32)
             nc.scalar.activation(result[:], negated[:], GELU, bias=no_bias[:], scale=-1.0)
@@ -192,7 +207,7 @@ def tile_picked_zeropt_gelu_l_kernel(tc, xT, zp, csum, w1, offs, out):
         for b in range(BLOCKS):
             for piece in LATE:
                 multiply(0, piece, b)
-        table = round_pairs(1, 1, tile("table11", [P, T], U32)[:])
+        table = round_pairs_in_two(1, 1, tile("table11", [P, T], U32)[:])
         for piece in LATE:
             gather(1, 1, piece, table)
         grouped = tile("w_grouped1", [P, N, PACK], BF16)[:]
@@ -207,4 +222,9 @@ def tile_picked_zeropt_gelu_l_kernel(tc, xT, zp, csum, w1, offs, out):
                 multiply(1, piece, b)
         for piece in LATE:
             for b in range(BLOCKS):
-                finish(piece, b)
+                lo, hi = piece
+                if (piece, b) == (LATE[-1], BLOCKS - 1):
+                    finish(piece, b, lo, hi - P)
+                    finish(piece, b, hi - P, hi)
+                else:
+                    finish(piece, b, lo, hi)

from contextlib import ExitStack

import concourse.mybir as mybir
from concourse.masks import make_identity

K, T, S, N = 1024, 1024, 512, 256
FLOPS = 2 * K * S * N

F32 = mybir.dt.float32
BF16 = mybir.dt.bfloat16
I32 = mybir.dt.int32
U32 = mybir.dt.uint32
U16 = mybir.dt.uint16
U8 = mybir.dt.uint8
FP8X4 = mybir.dt.float8_e4m3fn_x4
GELU = mybir.ActivationFunctionType.Gelu_apprx_tanh
MULT = mybir.AluOpType.mult
SUBTRACT = mybir.AluOpType.subtract

P = 128
PACK = 4
K_PASS = P * PACK
PASSES = K // K_PASS
BLOCKS = N // P
VECTOR_COLS = (672, 672, 608, 736)
WHOLE = (0, S)
LATE = ((0, 256), (256, 512))


def tile_picked_zeropt_gelu_l_kernel(tc, xT, zp, csum, w1, offs, out):
    nc = tc.nc
    with ExitStack() as ctx:
        keep = ctx.enter_context(tc.tile_pool(name="keep", bufs=1))
        psum = ctx.enter_context(tc.psum_pool(name="psum", bufs=1))

        def tile(name, shape, dtype, tag=None):
            return keep.tile(shape, dtype, name=name, tag=tag or name, align_bytes=64)

        offsets = keep.tile([P, S // 16], U16, name="offsets")
        zp_table = tile("zp_table", [P, T], F32)
        nc.gpsimd.memset(zp_table[0 : P - 1, :], 0.0)
        nc.scalar.dma_start(zp_table[P - 1 : P, :], zp[0:1, :])
        nc.sync.dma_start(offsets[:], offs)
        x_rows = xT.rearrange("(g p u t) c -> g u p t c", g=PASSES, u=2, t=2)
        w_rows = w1.rearrange("(g p j) m -> g p j m", g=PASSES, j=PACK)
        x_raw = {}
        w_raw = {}

        def load_x(g, u):
            x_raw[g, u] = tile("x_raw%d%d" % (g, u), [P, 2, T], F32)
            nc.sync.dma_start(x_raw[g, u][:], x_rows[g, u])

        def load_x_in_two(g, u):
            split = VECTOR_COLS[2 * g + u]
            x_raw[g, u] = []
            for lo, hi in ((0, split), (split, T)):
                part = tile("x_raw%d%d_%d" % (g, u, lo), [P, 2, hi - lo], F32)
                nc.sync.dma_start(part[:], x_rows[g, u][:, :, lo:hi])
                x_raw[g, u].append(part)

        def load_w(g):
            w_raw[g] = tile("w_raw%d" % g, [P, PACK, N], F32)
            nc.sync.dma_start(w_raw[g][:], w_rows[g])

        load_x(0, 0)
        load_x(0, 1)
        load_x(1, 0)
        load_w(0)
        load_x_in_two(1, 1)
        load_w(1)
        weight = tile("weight", [P, BLOCKS], F32)
        with nc.allow_non_contiguous_dma(reason="one value a partition"):
            nc.sync.dma_start(weight[:], csum.rearrange("(b p) o -> p (b o)", p=P))

        zero = tile("zero", [P, 1], F32)
        nc.vector.memset(zero[:], 0.0)
        no_bias = tile("no_bias", [P, 1], F32)
        nc.scalar.activation(no_bias[:], zero[:], GELU)

        identity = tile("identity", [P, P], F32)
        make_identity(nc, identity[:])
        zp_row = tile("zp_row", [P, S], F32)
        nc.vector.tensor_copy(zp_row[:], zp_table[:].indirect(offsets[:]))
        turned = psum.tile([P, S // P, P], F32, name="turned")
        for c in range(S // P):
            nc.tensor.transpose(turned[:, c, :], zp_row[:, c * P : (c + 1) * P], identity[:])
        zp_cols = tile("zp_cols", [P, S // P], F32)
        nc.scalar.copy(zp_cols[:], turned[:, :, P - 1])
        spread = psum.tile([P, S // P, P], F32, name="spread")
        for c in range(S // P):
            nc.tensor.transpose(spread[:, c, :], zp_cols[:, c : c + 1].to_broadcast([P, P]), identity[:])

        picked = {}
        woven = {}
        x_codes = {}
        x_scales = {}
        w_codes = {}
        w_scales = {}
        acc = {}

        def round_pairs(g, u, table):
            pairs = table.bitcast(BF16).rearrange("p (c t) -> p c t", t=2)
            src = x_raw[g, u][:].rearrange("p t c -> p c t")
            split = VECTOR_COLS[2 * g + u]
            nc.scalar.copy(pairs[:, split:, :], src[:, split:, :])
            nc.vector.tensor_copy(pairs[:, :split, :], src[:, :split, :])
            return table

        def round_pairs_in_two(g, u, table):
            pairs = table.bitcast(BF16).rearrange("p (c t) -> p c t", t=2)
            split = VECTOR_COLS[2 * g + u]
            first, second = x_raw[g, u]
            nc.vector.tensor_copy(pairs[:, :split, :], first[:].rearrange("p t c -> p c t"))
            nc.scalar.copy(pairs[:, split:, :], second[:].rearrange("p t c -> p c t"))
            return table

        def gather(g, u, piece, table):
            lo, hi = piece
            if u == 0:
                picked[g, piece] = tile("picked%d_%d" % (g, lo), [P, 2, hi - lo], U32)
            nc.vector.tensor_copy(picked[g, piece][:, u, :], table.indirect(offsets[:, lo // 16 : hi // 16]))

        def weave(g, piece, on_scalar, dst=None):
            lo, hi = piece
            if dst is None:
                dst = tile("woven%d_%d" % (g, lo), [P, hi - lo, 2], U32)[:]
            woven[g, piece] = dst
            src = picked[g, piece][:]
            if on_scalar:
                nc.scalar.copy(dst, src.rearrange("p u s -> p s u"))
            else:
                nc.vector.tensor_copy(dst.bitcast(I32), src.bitcast(I32).rearrange("p u s -> p s u"))

        def quantise_x(g, piece, tag=None):
            lo, hi = piece
            codes = tile("x_codes%d_%d" % (g, lo), [P, hi - lo], U32, tag=tag)
            scales = tile("x_scales%d_%d" % (g, lo), [P, hi - lo], U8)
            nc.vector.quantize_mx(
                out=codes[:].bitcast(FP8X4),
                scales=scales[:],
                in_=woven[g, piece].rearrange("p s u -> p (s u)").bitcast(BF16),
            )
            for a, b in LATE:
                if lo <= a and b <= hi:
                    x_codes[g, (a, b)] = codes[:, a - lo : b - lo]
                    x_scales[g, (a, b)] = scales[:, a - lo : b - lo]

        def round_w(g, lo, hi, engine, grouped):
            dst = grouped[:, lo:hi, :].rearrange("p (c i) j -> p c j i", i=4)
            src = w_raw[g][:, :, lo:hi].rearrange("p j (c i) -> p c j i", i=4)
            if engine == "scalar":
                nc.scalar.copy(dst, src)
            elif engine == "vector":
                nc.vector.tensor_copy(dst, src)
            else:
                nc.gpsimd.tensor_copy(dst, src)

        def quantise_w(g, lo, hi, grouped, tag=None):
            codes = tile("w_codes%d_%d" % (g, lo), [P, hi - lo], U32, tag=tag)
            scales = tile("w_scales%d_%d" % (g, lo), [P, hi - lo], U8)
            nc.vector.quantize_mx(
                out=codes[:].bitcast(FP8X4),
                scales=scales[:],
                in_=grouped[:, lo:hi, :].rearrange("p m j -> p (m j)"),
            )
            for m in range(lo, hi, P):
                w_codes[g, m // P] = codes[:, m - lo : m - lo + P]
                w_scales[g, m // P] = scales[:, m - lo : m - lo + P]

        def multiply(g, piece, b):
            lo, hi = piece
            if g == 0:
                acc[b, piece] = psum.tile([P, hi - lo], F32, name="acc%d_%d" % (b, lo))
            nc.tensor.matmul_mx(
                out=acc[b, piece][:],
                lhsT=w_codes[g, b].bitcast(FP8X4),
                lhsT_scale=w_scales[g, b],
                rhs=x_codes[g, piece].bitcast(FP8X4),
                rhs_scale=x_scales[g, piece],
                start=(g == 0),
                stop=(g == PASSES - 1),
            )

        def finish(piece, b, lo, hi):
            negated = tile("negated%d_%d" % (b, lo), [P, hi - lo], F32)
            nc.vector.scalar_tensor_tensor(
                negated[:], zp_picked[:, lo:hi], weight[:, b : b + 1], acc[b, piece][:, lo - piece[0] : hi - piece[0]], MULT, SUBTRACT
            )
            result = tile("result%d_%d" % (b, lo), [P, hi - lo], F32)
            nc.scalar.activation(result[:], negated[:], GELU, bias=no_bias[:], scale=-1.0)
            nc.sync.dma_start(out[b * P : (b + 1) * P, lo:hi], result[:])

        table = round_pairs(0, 0, tile("table00", [P, T], U32)[:])
        gather(0, 0, WHOLE, table)
        table = round_pairs(0, 1, tile("table01", [P, T], U32)[:])
        zp_picked = tile("zp_picked", [P, S], F32, tag="table00")
        nc.scalar.copy(zp_picked[:], spread[:].rearrange("p c n -> p (c n)"))
        gather(0, 1, WHOLE, table)
        table = round_pairs(1, 0, tile("table10", [P, T], U32)[:])
        for piece in LATE:
            gather(1, 0, piece, table)
        weave(0, WHOLE, True, tile("woven0", [P, S, 2], U32, tag="x_raw10")[:])
        quantise_x(0, WHOLE)
        grouped = tile("w_grouped0", [P, N, PACK], BF16)[:]
        round_w(0, 0, N, "scalar", grouped)
        quantise_w(0, 0, N, grouped)
        for b in range(BLOCKS):
            for piece in LATE:
                multiply(0, piece, b)
        table = round_pairs_in_two(1, 1, tile("table11", [P, T], U32)[:])
        for piece in LATE:
            gather(1, 1, piece, table)
        grouped = tile("w_grouped1", [P, N, PACK], BF16)[:]
        round_w(1, 0, N, "scalar", grouped)
        weave(1, LATE[0], False)
        weave(1, LATE[1], True)
        quantise_w(1, 0, N, grouped)
        quantise_x(1, LATE[0], tag="w_raw1")
        quantise_x(1, LATE[1])
        for piece in LATE:
            for b in range(BLOCKS):
                multiply(1, piece, b)
        for piece in LATE:
            for b in range(BLOCKS):
                lo, hi = piece
                if (piece, b) == (LATE[-1], BLOCKS - 1):
                    finish(piece, b, lo, hi - P)
                    finish(piece, b, hi - P, hi)
                else:
                    finish(piece, b, lo, hi)
